import numpy as np
import ml_dtypes


def mxq(x, axis, fmt="e4m3"):
    dtype, down = {"e4m3": (ml_dtypes.float8_e4m3fn, 7), "e5m2": (ml_dtypes.float8_e5m2, 14)}[fmt]
    v = np.moveaxis(np.asarray(x, np.float32).astype(ml_dtypes.bfloat16).astype(np.float64), axis, -1)
    blocks = v.reshape(v.shape[:-1] + (-1, 32))
    amax = np.abs(blocks).max(-1, keepdims=True)
    byte = np.maximum(np.where(amax > 0, np.frexp(amax)[1] - 1 + 127, 0) - down, 1)
    scale = np.exp2(byte - 127.0)
    codes = (blocks / scale).astype(np.float32).astype(dtype).astype(np.float64)
    return np.moveaxis((codes * scale).reshape(v.shape), -1, axis)


WIDE = False


def mx_kscale(k):
    if not WIDE:
        return np.ones(k)
    levels = np.array([10, -10, 5, -5, 0])
    if k % 512:
        return np.exp2(np.random.permutation(np.resize(levels, k // 32))).repeat(32)
    a = np.empty((k // 512, 16))
    for p in range(k // 512):
        a[p, :8] = np.random.permutation(np.resize(levels, 8))
        for g in range(8):
            far = levels[np.abs(levels - a[p, g]) >= 10]
            a[p, g + 8] = far[np.random.randint(len(far))]
    return np.exp2(a.ravel()).repeat(32)


def f64(x):
    return np.asarray(x).astype(np.float64)


def striped(idx):
    return np.tile(idx.reshape(-1, 16).T, (8, 1)).astype(np.uint16)


def unstriped(offs):
    return offs[:16].T.reshape(-1).astype(np.int64)


def pack_weight(w):
    k, n = w.shape
    w = f64(np.asarray(w, np.float32).astype(ml_dtypes.bfloat16)).reshape(k // 32, 32, n)
    amax = np.abs(w).max(1)
    byte = np.clip(np.where(amax > 0, np.frexp(amax)[1] - 1 + 127 - 7, 1), 1, 254)
    scaled = (w * np.exp2(127.0 - byte)[:, None, :]).reshape(k, n).astype(np.float32)
    words = np.ascontiguousarray(scaled.reshape(k // 512, 128, 4, n).transpose(0, 1, 3, 2)).astype(ml_dtypes.float8_e4m3fn).view(np.uint8)
    return words, np.ascontiguousarray(byte.astype(np.uint8).reshape(k // 512, 16, n))


def unpack_weight(words, scales):
    g, p, n, _ = words.shape
    vals = np.ascontiguousarray(words).view(ml_dtypes.float8_e4m3fn).astype(np.float64) * np.repeat(np.exp2(scales.astype(np.float64) - 127.0), 8, axis=1)[..., None]
    return vals.transpose(0, 1, 3, 2).reshape(g * 512, n)


def planes(y):
    n, m = y.shape
    v = y.astype(np.float32).astype(ml_dtypes.bfloat16).astype(np.float64).reshape(n // 32, 32, m)
    top = np.abs(v).max(1)
    byte = np.clip(np.where(top > 0, np.frexp(top)[1] - 1 + 127 - 7, 1), 1, 254)
    codes = (v * np.exp2(127.0 - byte)[:, None, :]).reshape(n, m).astype(np.float32).astype(ml_dtypes.float8_e4m3fn).view(np.uint8)
    words = codes.reshape(n // 512, 128, 4, m).transpose(0, 1, 3, 2)
    return np.ascontiguousarray(words), np.ascontiguousarray(byte.astype(np.uint8).reshape(n // 512, 16, m))


K, T, S, D, H, N = 512, 1024, 512, 8, 512, 512


def setup_inputs():
    n = np.random.standard_normal
    s = mx_kscale(K)[:, None]
    u = mx_kscale(H)
    packed_xT = pack_weight(n((K, T)) * s)
    packed_eT = pack_weight(n((K, T)) * s)
    return {
        "x_words": packed_xT[0],
        "x_scales": packed_xT[1],
        "e_words": packed_eT[0],
        "e_scales": packed_eT[1],
        "w1": (n((K, N)) / np.sqrt(K) / s).astype(np.float32),
        "unit": (np.random.uniform(0.7, 1.3, (H, 1)) * u[:, None]).astype(np.float32),
        "w2": (n((H, N)) / np.sqrt(H) / u[:, None]).astype(np.float32),
        "offs": striped(np.random.permutation(T)[:S]),
    }


def reference(x_words, x_scales, e_words, e_scales, w1, unit, w2, offs):
    e_offs = unpack_weight(e_words, e_scales)[:, unstriped(offs)]
    w1q = mxq(f64(w1), 0, "e4m3")
    h = w1q.T @ e_offs
    mb = h.reshape(len(h), -1, D).mean(axis=2)
    g0 = ((mb) ** 2) / ((mb) ** 2 + 0.2)
    xq = unpack_weight(x_words, x_scales)[:, unstriped(offs)]
    y = w1q.T @ xq
    mc = y.reshape(len(y), -1, D).mean(axis=2)
    gm = g0 * mc
    d2 = (h - np.repeat(mb, D, axis=1)) ** 2
    vb = d2.reshape(len(d2), -1, D).mean(axis=2)
    g1 = vb / (vb + 0.3)
    z = f64(unit) * (np.repeat(gm, D, axis=1) + np.repeat(g1, D, axis=1) * (y - np.repeat(mc, D, axis=1)))
    out_0 = mxq(f64(w2), 0, "e4m3").T @ mxq(z, 0, "e4m3")
    return (out_0,) + planes(out_0)

@@ -1,0 +1,294 @@
+import math
+from contextlib import ExitStack
+
+import concourse.mybir as mybir
+from concourse.masks import make_identity
+
+K, T, S, D, H, N = 512, 1024, 512, 8, 512, 512
+FLOPS = 3 * 2 * 512 * 512 * 512
+
+F32 = mybir.dt.float32
+BF16 = mybir.dt.bfloat16
+I32 = mybir.dt.int32
+U32 = mybir.dt.uint32
+U16 = mybir.dt.uint16
+U8 = mybir.dt.uint8
+FP8X4 = mybir.dt.float8_e4m3fn_x4
+ALU = mybir.AluOpType
+ACT = mybir.ActivationFunctionType
+AX = mybir.AxisListType
+
+P = 128
+PACK = 4
+HALF = 256
+CH = 128
+GV = CH // D
+C0 = 1.0 / (D * math.sqrt(0.2))
+C1 = 1.0 / (D * math.sqrt(D * 0.3))
+
+
+def tile_picked_ywien_wien_po_kernel(
+    tc, x_words, x_scales, e_words, e_scales, w1, unit, w2, offs, out_0, out_1, out_2
+):
+    nc = tc.nc
+    with ExitStack() as ctx:
+        held = ctx.enter_context(tc.tile_pool(name="held", bufs=1))
+        psum = ctx.enter_context(tc.psum_pool(name="psum", bufs=1))
+
+        def sb(name, shape, dtype):
+            return held.tile(shape, dtype, name=name, align_bytes=64)
+
+        def bank(k, name):
+            return psum.tile([P, 512], F32, name=name, tag="bank%d" % k)
+
+        offsets = held.tile([P, S // 16], U16, name="offsets")
+        nc.sync.dma_start(offsets[:], offs)
+
+        e_sc = sb("e_sc", [P, T], U8)
+        x_sc = sb("x_sc", [P, T], U8)
+        nc.vector.memset(e_sc[:].bitcast(I32), 0)
+        nc.vector.memset(x_sc[:].bitcast(I32), 0)
+        warm_in = sb("warm_in", [P, 1], F32)
+        warm_out = sb("warm_out", [P, 1], F32)
+        nc.vector.memset(warm_in[:], 1.0)
+        for q in range(4):
+            nc.scalar.dma_start(e_sc[32 * q : 32 * q + 4, :].bitcast(I32), e_scales[0, 4 * q : 4 * q + 4, :].bitcast(I32))
+        nc.scalar.activation(warm_out[:], warm_in[:], ACT.Abs_reciprocal_sqrt)
+        for q in range(4):
+            nc.gpsimd.dma_start(x_sc[32 * q : 32 * q + 4, :].bitcast(I32), x_scales[0, 4 * q : 4 * q + 4, :].bitcast(I32))
+        w1_rows = w1.rearrange("(p j) c -> p j c", j=PACK)
+        w2_rows = w2.rearrange("(p j) c -> p j c", j=PACK)
+        w1_raw = []
+        for a in range(2):
+            raw = sb("w1_raw%d" % a, [P, PACK, 256], F32)
+            nc.sync.dma_start(raw[:], w1_rows[:, :, 256 * a : 256 * (a + 1)])
+            w1_raw.append(raw)
+        e_w = sb("e_w", [P, T], U32)
+        nc.sync.dma_start(e_w[:].bitcast(I32), e_words[0].rearrange("p n t -> p (n t)").bitcast(I32))
+        x_w = sb("x_w", [P, T], U32)
+        nc.sync.dma_start(x_w[:].bitcast(I32), x_words[0].rearrange("p n t -> p (n t)").bitcast(I32))
+        w2_raw = sb("w2_raw", [P, PACK, N], F32)
+        nc.sync.dma_start(w2_raw[:], w2_rows)
+        gain = sb("gain", [P, PACK], F32)
+        nc.sync.dma_start(gain[:], unit.rearrange("(p t) o -> p (t o)", t=PACK))
+        ident = sb("ident", [P, P], F32)
+        make_identity(nc, ident[:])
+
+        e_gs = sb("e_gs", [P, S], U8)
+        x_gs = sb("x_gs", [P, S], U8)
+        nc.vector.tensor_copy(e_gs[:], e_sc[:].indirect(offsets[:]))
+        nc.vector.tensor_copy(x_gs[:], x_sc[:].indirect(offsets[:]))
+
+        w1_bf = sb("w1_bf", [P, PACK, P, PACK], BF16)
+        for a in range(2):
+            nc.scalar.copy(
+                w1_bf[:, :, 64 * a : 64 * (a + 1), :].rearrange("p t m j -> p m j t"),
+                w1_raw[a][:].rearrange("p j (m t) -> p m j t", t=PACK),
+            )
+
+        def gather_words(name, table, half):
+            g = sb(name, [P, HALF], U32)
+            nc.vector.tensor_copy(g[:], table[:].indirect(offsets[:, 16 * half : 16 * (half + 1)]))
+            return g
+
+        def quantize(codes, scales, values):
+            nc.vector.quantize_mx(out=codes.bitcast(FP8X4), scales=scales, in_=values)
+
+        def product(dst, w_codes, w_scales, codes, scales):
+            for t in range(PACK):
+                cols = slice(P * t, P * (t + 1))
+                nc.tensor.matmul_mx(
+                    out=dst[:, cols],
+                    lhsT=w_codes[:, cols].bitcast(FP8X4),
+                    lhsT_scale=w_scales[:, cols],
+                    rhs=codes.bitcast(FP8X4),
+                    rhs_scale=scales,
+                    start=True,
+                    stop=True,
+                )
+
+        e_g = [gather_words("e_g0", e_w, 0)]
+        w1_c = sb("w1_c", [P, N], U32)
+        w1_s = sb("w1_s", [P, N], U8)
+        quantize(w1_c[:], w1_s[:], w1_bf[:].rearrange("p t m j -> p (t m j)"))
+        e_g.append(gather_words("e_g1", e_w, 1))
+
+        def first_product(name, banks, g, gs, half):
+            res = []
+            for b in range(2):
+                dst = bank(banks[b], "%s%d%d" % (name, half, b))
+                product(dst, w1_c, w1_s, g[:, CH * b : CH * (b + 1)], gs[:, HALF * half + CH * b : HALF * half + CH * (b + 1)])
+                res.append(dst)
+            return res
+
+        hsum = [sb("hsum%d" % k, [P, 128], F32) for k in range(2)]
+        hneg = [sb("hneg%d" % k, [P, D, 128], F32) for k in range(2)]
+        sq = [sb("sq%d" % k, [P, D, 128], F32) for k in range(2)]
+        ysum = [sb("ysum%d" % k, [P, 128], F32) for k in range(2)]
+
+        def h_sums(h, half):
+            for b in range(2):
+                nc.vector.tensor_reduce(
+                    hsum[half][:, 64 * b : 64 * (b + 1)], h[b][:].rearrange("p (c d) -> p c d", d=D), AX.X, ALU.add
+                )
+                o = 1 - b
+                nc.scalar.activation(
+                    hneg[half][:, :, 64 * o : 64 * (o + 1)], h[o][:].rearrange("p (c d) -> p d c", d=D), ACT.Copy, scale=-8.0
+                )
+
+        def deviations(half, banks):
+            for u in range(2):
+                dh = bank(banks[u], "dh%d%d" % (half, u))
+                for d4 in range(4):
+                    cols = slice(P * d4, P * (d4 + 1))
+                    nc.tensor.matmul(dh[:, cols], hneg[half][:, 4 * u + d4, :], ident[:], start=True, stop=False, is_transpose=True)
+                    nc.tensor.matmul(dh[:, cols], hsum[half][:], ident[:], start=False, stop=True, is_transpose=True)
+                nc.scalar.activation(
+                    sq[half][:, 4 * u : 4 * (u + 1), :].rearrange("p d c -> p (d c)"), dh[:], ACT.Square, scale=C1
+                )
+
+        def spread(half, k):
+            qb = bank(k, "q%d" % half)
+            for d in range(D):
+                nc.tensor.matmul(qb[:, 0:128], sq[half][:, d, :], ident[:], start=(d == 0), stop=(d == D - 1), is_transpose=True)
+            return qb
+
+        def y_sums(y, half):
+            for b in range(2):
+                nc.vector.tensor_reduce(
+                    ysum[half][:, 64 * b : 64 * (b + 1)].rearrange("p (v t) -> p t v", t=PACK),
+                    y[b][:].rearrange("p (t v d) -> p t v d", t=PACK, d=D),
+                    AX.X,
+                    ALU.add,
+                )
+
+        def shrink(name, x):
+            q = sb(name + "_q", [P, 128], F32)
+            r = sb(name + "_r", [P, 128], F32)
+            g = sb(name + "_g", [P, 128], F32)
+            nc.scalar.activation(q[:], x, ACT.Abs_reciprocal_sqrt, bias=1.0)
+            nc.scalar.activation(
+                r[:].rearrange("p (b v t) -> p b v t", b=2, t=PACK), q[:].rearrange("p (b t v) -> p b v t", b=2, t=PACK), ACT.Square
+            )
+            nc.vector.tensor_tensor(
+                g[:].rearrange("p (b v t) -> p b v t", b=2, t=PACK),
+                x.rearrange("p (b t v) -> p b v t", b=2, t=PACK),
+                r[:].rearrange("p (b v t) -> p b v t", b=2, t=PACK),
+                ALU.mult,
+            )
+            return g
+
+        def mean_gain(half):
+            x0 = sb("x0_%d" % half, [P, 128], F32)
+            nc.scalar.activation(x0[:], hsum[half][:], ACT.Square, scale=C0)
+            return shrink("g0_%d" % half, x0[:])
+
+        gain_b = gain[:].rearrange("p (o t) -> p o t", o=1).to_broadcast([P, 32, PACK])
+
+        def by_t(ap):
+            return ap.rearrange("p (c t) -> p c t", t=PACK)
+
+        def factors(half, g0, qb):
+            ym = sb("ym%d" % half, [P, 128], F32)
+            nc.vector.scalar_tensor_tensor(by_t(ym[:]), by_t(ysum[half][:]), 1.0 / D, gain_b, ALU.mult, ALU.mult)
+            g1 = shrink("g1_%d" % half, qb[:, 0:128])
+            slope = sb("slope%d" % half, [P, 128], F32)
+            nc.vector.tensor_tensor(by_t(slope[:]), by_t(g1[:]), gain_b, ALU.mult)
+            diff = sb("diff%d" % half, [P, 128], F32)
+            nc.vector.tensor_tensor(diff[:], g0[:], g1[:], ALU.subtract)
+            shift = sb("shift%d" % half, [P, 128], F32)
+            nc.vector.tensor_tensor(shift[:], diff[:], ym[:], ALU.mult)
+            return slope, shift
+
+        def over_group(ap, b):
+            return ap[:, 64 * b : 64 * (b + 1)].rearrange("p (v o t) -> p v o t", o=1, t=PACK).to_broadcast([P, GV, D, PACK])
+
+        def vdt(ap):
+            return ap.rearrange("p (v d t) -> p v d t", d=D, t=PACK)
+
+        def scaled(c, yb, slope):
+            u = sb("u%d" % c, [P, 512], F32)
+            nc.vector.tensor_tensor(
+                vdt(u[:]), yb[:].rearrange("p (t v d) -> p v d t", t=PACK, d=D), over_group(slope, c % 2), ALU.mult
+            )
+            return u
+
+        def shifted(c, u, shift):
+            z = sb("z%d" % c, [P, 512], BF16)
+            eng = nc.gpsimd if c in () else nc.vector
+            eng.tensor_tensor(vdt(z[:]), vdt(u[:]), over_group(shift, c % 2), ALU.add)
+            return z
+
+        out_rows = out_0.rearrange("(p t) j -> p t j", t=PACK)
+        o_c = sb("o_c", [P, S], U32)
+        o_s = sb("o_s", [P, S], U8)
+        out_words = out_1[0].rearrange("p n t -> p (n t)").bitcast(I32)
+
+        def second_product(c, z, k):
+            z_c = sb("z_c%d" % c, [P, CH], U32)
+            z_s = sb("z_s%d" % c, [P, CH], U8)
+            quantize(z_c[:], z_s[:], z[:])
+            dst = bank(k, "o%d" % c)
+            product(dst, w2_c, w2_s, z_c[:], z_s[:])
+            o32 = sb("o32_%d" % c, [P, PACK, CH], F32)
+            nc.scalar.copy(o32[:].rearrange("p t j -> p (t j)"), dst[:])
+            nc.sync.dma_start(out_rows[:, :, CH * c : CH * (c + 1)], o32[:])
+            o16 = sb("o16_%d" % c, [P, CH, PACK], BF16)
+            nc.scalar.copy(o16[:], dst[:].rearrange("p (t j) -> p j t", t=PACK))
+            return o16
+
+        def planes(c, o16):
+            cols = slice(CH * c, CH * (c + 1))
+            quantize(o_c[:, cols], o_s[:, cols], o16[:].rearrange("p j t -> p (j t)"))
+            if c % 2 == 1:
+                cols = slice(CH * (c - 1), CH * (c + 1))
+                nc.sync.dma_start(out_words[:, cols], o_c[:, cols].bitcast(I32))
+
+        h0 = first_product("h", (0, 1), e_g[0], e_gs, 0)
+        h1 = first_product("h", (2, 3), e_g[1], e_gs, 1)
+        h_sums(h0, 0)
+        x_g0 = gather_words("x_g0", x_w, 0)
+        deviations(0, (4, 5))
+        h_sums(h1, 1)
+        y0 = first_product("y", (6, 7), x_g0, x_gs, 0)
+        x_g1 = gather_words("x_g1", x_w, 1)
+        q0 = spread(0, 0)
+        deviations(1, (4, 5))
+        y_sums(y0, 0)
+        g00 = mean_gain(0)
+        y1 = first_product("y", (2, 3), x_g1, x_gs, 1)
+
+        w2_bf = sb("w2_bf", [P, PACK, P, PACK], BF16)
+        for a in range(2):
+            nc.scalar.copy(
+                w2_bf[:, :, 64 * a : 64 * (a + 1), :].rearrange("p t m j -> p m j t"),
+                w2_raw[:, :, 256 * a : 256 * (a + 1)].rearrange("p j (m t) -> p m j t", t=PACK),
+            )
+        slope0, shift0 = factors(0, g00, q0)
+        q1 = spread(1, 1)
+        g01 = mean_gain(1)
+        y_sums(y1, 1)
+        w2_c = sb("w2_c", [P, N], U32)
+        w2_s = sb("w2_s", [P, N], U8)
+        quantize(w2_c[:], w2_s[:], w2_bf[:].rearrange("p t m j -> p (t m j)"))
+
+        u0 = scaled(0, y0[0], slope0)
+        u1 = scaled(1, y0[1], slope0)
+        z0 = shifted(0, u0, shift0)
+        z1 = shifted(1, u1, shift0)
+        slope1, shift1 = factors(1, g01, q1)
+        o0 = second_product(0, z0, 4)
+        o1 = second_product(1, z1, 5)
+        u2 = scaled(2, y1[0], slope1)
+        u3 = scaled(3, y1[1], slope1)
+        z2 = shifted(2, u2, shift1)
+        z3 = shifted(3, u3, shift1)
+        o2 = second_product(2, z2, 6)
+        planes(0, o0)
+        o3 = second_product(3, z3, 7)
+        planes(1, o1)
+        planes(2, o2)
+        planes(3, o3)
+        for q in range(4):
+            eng = nc.sync if q % 2 == 0 else nc.scalar
+            eng.dma_start(out_2[0, 4 * q : 4 * q + 4, :].bitcast(I32), o_s[32 * q : 32 * q + 4, :].bitcast(I32))

@@ -51,24 +51,36 @@ def tile_picked_ywien_wien_po_kernel(
         warm_in = sb("warm_in", [P, 1], F32)
         warm_out = sb("warm_out", [P, 1], F32)
         nc.vector.memset(warm_in[:], 1.0)
-        for q in range(4):
-            nc.scalar.dma_start(e_sc[32 * q : 32 * q + 4, :].bitcast(I32), e_scales[0, 4 * q : 4 * q + 4, :].bitcast(I32))
         nc.scalar.activation(warm_out[:], warm_in[:], ACT.Abs_reciprocal_sqrt)
-        for q in range(4):
-            nc.gpsimd.dma_start(x_sc[32 * q : 32 * q + 4, :].bitcast(I32), x_scales[0, 4 * q : 4 * q + 4, :].bitcast(I32))
-        w1_rows = w1.rearrange("(p j) c -> p j c", j=PACK)
-        w2_rows = w2.rearrange("(p j) c -> p j c", j=PACK)
-        w1_raw = []
-        for a in range(2):
-            raw = sb("w1_raw%d" % a, [P, PACK, 256], F32)
-            nc.sync.dma_start(raw[:], w1_rows[:, :, 256 * a : 256 * (a + 1)])
-            w1_raw.append(raw)
-        e_w = sb("e_w", [P, T], U32)
-        nc.sync.dma_start(e_w[:].bitcast(I32), e_words[0].rearrange("p n t -> p (n t)").bitcast(I32))
-        x_w = sb("x_w", [P, T], U32)
-        nc.sync.dma_start(x_w[:].bitcast(I32), x_words[0].rearrange("p n t -> p (n t)").bitcast(I32))
-        w2_raw = sb("w2_raw", [P, PACK, N], F32)
-        nc.sync.dma_start(w2_raw[:], w2_rows)
+
+        def load_weight(name, w, a):
+            raw = held.tile([P, PACK, 256], F32, name="%s_raw%d" % (name, a), align_bytes=64)
+            nc.sync.dma_start(raw[:], w.rearrange("(p j) c -> p j c", j=PACK)[:, :, 256 * a : 256 * (a + 1)])
+            return raw
+
+        def round_weight(dst, raw, a, lo, hi, copy=nc.scalar.copy):
+            copy(
+                dst[:, :, 64 * a + lo : 64 * a + hi, :].rearrange("p t m j -> p m j t"),
+                raw[:, :, PACK * lo : PACK * hi].rearrange("p j (m t) -> p m j t", t=PACK),
+            )
+
+        def load_scales(dst, src):
+            for q in range(4):
+                nc.sync.dma_start(dst[32 * q : 32 * q + 4, :].bitcast(I32), src[0, 4 * q : 4 * q + 4, :].bitcast(I32))
+
+        def load_words(name, src):
+            dst = sb(name, [P, T], U32)
+            nc.sync.dma_start(dst[:].bitcast(I32), src[0].rearrange("p n t -> p (n t)").bitcast(I32))
+            return dst
+
+        w1_raw = [load_weight("w1", w1, 0)]
+        load_scales(e_sc, e_scales)
+        w1_raw.append(load_weight("w1", w1, 1))
+        e_w = load_words("e_w", e_words)
+        load_scales(x_sc, x_scales)
+        w2_raw = [load_weight("w2", w2, 0)]
+        x_w = load_words("x_w", x_words)
+        w2_raw.append(load_weight("w2", w2, 1))
         gain = sb("gain", [P, PACK], F32)
         nc.sync.dma_start(gain[:], unit.rearrange("(p t) o -> p (t o)", t=PACK))
         ident = sb("ident", [P, P], F32)
@@ -77,14 +89,10 @@ def tile_picked_ywien_wien_po_kernel(
         e_gs = sb("e_gs", [P, S], U8)
         x_gs = sb("x_gs", [P, S], U8)
         nc.vector.tensor_copy(e_gs[:], e_sc[:].indirect(offsets[:]))
-        nc.vector.tensor_copy(x_gs[:], x_sc[:].indirect(offsets[:]))
 
         w1_bf = sb("w1_bf", [P, PACK, P, PACK], BF16)
-        for a in range(2):
-            nc.scalar.copy(
-                w1_bf[:, :, 64 * a : 64 * (a + 1), :].rearrange("p t m j -> p m j t"),
-                w1_raw[a][:].rearrange("p j (m t) -> p m j t", t=PACK),
-            )
+        round_weight(w1_bf, w1_raw[0], 0, 0, 64)
+        round_weight(w1_bf, w1_raw[1], 1, 0, 64, nc.vector.tensor_copy)
 
         def gather_words(name, table, half):
             g = sb(name, [P, HALF], U32)
@@ -121,7 +129,8 @@ def tile_picked_ywien_wien_po_kernel(
                 res.append(dst)
             return res
 
-        hsum = [sb("hsum%d" % k, [P, 128], F32) for k in range(2)]
+        hsum_all = sb("hsum", [P, 256], F32)
+        hsum = [hsum_all[:, 128 * k : 128 * (k + 1)] for k in range(2)]
         hneg = [sb("hneg%d" % k, [P, D, 128], F32) for k in range(2)]
         sq = [sb("sq%d" % k, [P, D, 128], F32) for k in range(2)]
         ysum = [sb("ysum%d" % k, [P, 128], F32) for k in range(2)]
@@ -142,7 +151,7 @@ def tile_picked_ywien_wien_po_kernel(
                 for d4 in range(4):
                     cols = slice(P * d4, P * (d4 + 1))
                     nc.tensor.matmul(dh[:, cols], hneg[half][:, 4 * u + d4, :], ident[:], start=True, stop=False, is_transpose=True)
-                    nc.tensor.matmul(dh[:, cols], hsum[half][:], ident[:], start=False, stop=True, is_transpose=True)
+                    nc.tensor.matmul(dh[:, cols], hsum[half], ident[:], start=False, stop=True, is_transpose=True)
                 nc.scalar.activation(
                     sq[half][:, 4 * u : 4 * (u + 1), :].rearrange("p d c -> p (d c)"), dh[:], ACT.Square, scale=C1
                 )
@@ -162,42 +171,44 @@ def tile_picked_ywien_wien_po_kernel(
                     ALU.add,
                 )
 
-        def shrink(name, x):
-            q = sb(name + "_q", [P, 128], F32)
-            r = sb(name + "_r", [P, 128], F32)
-            g = sb(name + "_g", [P, 128], F32)
+        def shrink(name, x, nb, eng):
+            q = sb(name + "_q", [P, 64 * nb], F32)
+            r = sb(name + "_r", [P, 64 * nb], F32)
+            g = sb(name + "_g", [P, 64 * nb], F32)
             nc.scalar.activation(q[:], x, ACT.Abs_reciprocal_sqrt, bias=1.0)
-            nc.scalar.activation(
-                r[:].rearrange("p (b v t) -> p b v t", b=2, t=PACK), q[:].rearrange("p (b t v) -> p b v t", b=2, t=PACK), ACT.Square
-            )
-            nc.vector.tensor_tensor(
-                g[:].rearrange("p (b v t) -> p b v t", b=2, t=PACK),
-                x.rearrange("p (b t v) -> p b v t", b=2, t=PACK),
-                r[:].rearrange("p (b v t) -> p b v t", b=2, t=PACK),
+            nc.scalar.activation(r[:], q[:], ACT.Square)
+            eng.tensor_tensor(
+                g[:].rearrange("p (b v t) -> p b v t", b=nb, t=PACK),
+                x.rearrange("p (b t v) -> p b v t", b=nb, t=PACK),
+                r[:].rearrange("p (b t v) -> p b v t", b=nb, t=PACK),
                 ALU.mult,
             )
             return g
 
-        def mean_gain(half):
-            x0 = sb("x0_%d" % half, [P, 128], F32)
-            nc.scalar.activation(x0[:], hsum[half][:], ACT.Square, scale=C0)
-            return shrink("g0_%d" % half, x0[:])
+        def mean_gain():
+            x0 = sb("x0", [P, 256], F32)
+            nc.scalar.activation(x0[:], hsum_all[:], ACT.Square, scale=C0)
+            return shrink("g0", x0[:], 4, nc.gpsimd)
 
-        gain_b = gain[:].rearrange("p (o t) -> p o t", o=1).to_broadcast([P, 32, PACK])
+        gain8 = sb("gain8", [P, PACK], F32)
+        nc.gpsimd.tensor_scalar(gain8[:], gain[:], 1.0 / D, 0.0, ALU.mult, ALU.add)
+
+        def along_groups(ap):
+            return ap.rearrange("p (o t) -> p o t", o=1).to_broadcast([P, 32, PACK])
 
         def by_t(ap):
             return ap.rearrange("p (c t) -> p c t", t=PACK)
 
         def factors(half, g0, qb):
             ym = sb("ym%d" % half, [P, 128], F32)
-            nc.vector.scalar_tensor_tensor(by_t(ym[:]), by_t(ysum[half][:]), 1.0 / D, gain_b, ALU.mult, ALU.mult)
-            g1 = shrink("g1_%d" % half, qb[:, 0:128])
+            nc.gpsimd.tensor_tensor(by_t(ym[:]), by_t(ysum[half][:]), along_groups(gain8[:]), ALU.mult)
+            g1 = shrink("g1_%d" % half, qb[:, 0:128], 2, nc.vector)
             slope = sb("slope%d" % half, [P, 128], F32)
-            nc.vector.tensor_tensor(by_t(slope[:]), by_t(g1[:]), gain_b, ALU.mult)
+            nc.vector.tensor_tensor(by_t(slope[:]), by_t(g1[:]), along_groups(gain[:]), ALU.mult)
             diff = sb("diff%d" % half, [P, 128], F32)
-            nc.vector.tensor_tensor(diff[:], g0[:], g1[:], ALU.subtract)
+            nc.gpsimd.tensor_tensor(diff[:], g0[:, 128 * half : 128 * (half + 1)], g1[:], ALU.subtract)
             shift = sb("shift%d" % half, [P, 128], F32)
-            nc.vector.tensor_tensor(shift[:], diff[:], ym[:], ALU.mult)
+            nc.gpsimd.tensor_tensor(shift[:], diff[:], ym[:], ALU.mult)
             return slope, shift
 
         def over_group(ap, b):
@@ -230,65 +241,61 @@ def tile_picked_ywien_wien_po_kernel(
             quantize(z_c[:], z_s[:], z[:])
             dst = bank(k, "o%d" % c)
             product(dst, w2_c, w2_s, z_c[:], z_s[:])
+            o16 = sb("o16_%d" % c, [P, CH, PACK], BF16)
             o32 = sb("o32_%d" % c, [P, PACK, CH], F32)
             nc.scalar.copy(o32[:].rearrange("p t j -> p (t j)"), dst[:])
             nc.sync.dma_start(out_rows[:, :, CH * c : CH * (c + 1)], o32[:])
-            o16 = sb("o16_%d" % c, [P, CH, PACK], BF16)
-            nc.scalar.copy(o16[:], dst[:].rearrange("p (t j) -> p j t", t=PACK))
+            if c in (2,3):
+                nc.vector.tensor_copy(
+                    o16[:].rearrange("p (c i) t -> p c t i", i=4), o32[:].rearrange("p t (c i) -> p c t i", i=4)
+                )
+            else:
+                nc.scalar.copy(o16[:], dst[:].rearrange("p (t j) -> p j t", t=PACK))
             return o16
 
         def planes(c, o16):
             cols = slice(CH * c, CH * (c + 1))
             quantize(o_c[:, cols], o_s[:, cols], o16[:].rearrange("p j t -> p (j t)"))
-            if c % 2 == 1:
-                cols = slice(CH * (c - 1), CH * (c + 1))
+            if c >= 2:
+                cols = slice(0, 3 * CH) if c == 2 else cols
                 nc.sync.dma_start(out_words[:, cols], o_c[:, cols].bitcast(I32))
+
+        def gather_scales(half):
+            nc.vector.tensor_copy(x_gs[:, HALF * half : HALF * (half + 1)], x_sc[:].indirect(offsets[:, 16 * half : 16 * (half + 1)]))
 
         h0 = first_product("h", (0, 1), e_g[0], e_gs, 0)
         h1 = first_product("h", (2, 3), e_g[1], e_gs, 1)
         h_sums(h0, 0)
-        x_g0 = gather_words("x_g0", x_w, 0)
         deviations(0, (4, 5))
         h_sums(h1, 1)
+        q0 = spread(0, 4)
+        gather_scales(0)
+        x_g0 = gather_words("x_g0", x_w, 0)
         y0 = first_product("y", (6, 7), x_g0, x_gs, 0)
+        deviations(1, (0, 1))
+        gather_scales(1)
         x_g1 = gather_words("x_g1", x_w, 1)
-        q0 = spread(0, 0)
-        deviations(1, (4, 5))
-        y_sums(y0, 0)
-        g00 = mean_gain(0)
+        q1 = spread(1, 5)
         y1 = first_product("y", (2, 3), x_g1, x_gs, 1)
-
+        y_sums(y0, 0)
+        g0 = mean_gain()
+        slope0, shift0 = factors(0, g0, q0)
         w2_bf = sb("w2_bf", [P, PACK, P, PACK], BF16)
         for a in range(2):
-            nc.scalar.copy(
-                w2_bf[:, :, 64 * a : 64 * (a + 1), :].rearrange("p t m j -> p m j t"),
-                w2_raw[:, :, 256 * a : 256 * (a + 1)].rearrange("p j (m t) -> p m j t", t=PACK),
-            )
-        slope0, shift0 = factors(0, g00, q0)
-        q1 = spread(1, 1)
-        g01 = mean_gain(1)
-        y_sums(y1, 1)
+            round_weight(w2_bf, w2_raw[a], a, 0, 32)
+            round_weight(w2_bf, w2_raw[a], a, 32, 64)
         w2_c = sb("w2_c", [P, N], U32)
         w2_s = sb("w2_s", [P, N], U8)
         quantize(w2_c[:], w2_s[:], w2_bf[:].rearrange("p t m j -> p (t m j)"))
-
-        u0 = scaled(0, y0[0], slope0)
-        u1 = scaled(1, y0[1], slope0)
-        z0 = shifted(0, u0, shift0)
-        z1 = shifted(1, u1, shift0)
-        slope1, shift1 = factors(1, g01, q1)
-        o0 = second_product(0, z0, 4)
-        o1 = second_product(1, z1, 5)
-        u2 = scaled(2, y1[0], slope1)
-        u3 = scaled(3, y1[1], slope1)
-        z2 = shifted(2, u2, shift1)
-        z3 = shifted(3, u3, shift1)
-        o2 = second_product(2, z2, 6)
-        planes(0, o0)
-        o3 = second_product(3, z3, 7)
-        planes(1, o1)
-        planes(2, o2)
-        planes(3, o3)
+        o = []
+        for c in range(2):
+            o.append(second_product(c, shifted(c, scaled(c, y0[c], slope0), shift0), c))
+        y_sums(y1, 1)
+        slope1, shift1 = factors(1, g0, q1)
+        for c in range(2, 4):
+            o.append(second_product(c, shifted(c, scaled(c, y1[c - 2], slope1), shift1), 4 + c))
+        for c in range(4):
+            planes(c, o[c])
         for q in range(4):
             eng = nc.sync if q % 2 == 0 else nc.scalar
             eng.dma_start(out_2[0, 4 * q : 4 * q + 4, :].bitcast(I32), o_s[32 * q : 32 * q + 4, :].bitcast(I32))

@@ -156,10 +156,35 @@ def tile_picked_ywien_wien_po_kernel(
                     sq[half][:, 4 * u : 4 * (u + 1), :].rearrange("p d c -> p (d c)"), dh[:], ACT.Square, scale=C1
                 )
 
+        def h_sums_direct(h, half):
+            dev = sb("dev%d" % half, [P, D, 128], F32)
+            for b in range(2):
+                nc.vector.tensor_reduce(
+                    hsum[half][:, 64 * b : 64 * (b + 1)], h[b][:].rearrange("p (c d) -> p c d", d=D), AX.X, ALU.add
+                )
+            for b in range(2):
+                cols = slice(64 * b, 64 * (b + 1))
+                nc.vector.scalar_tensor_tensor(
+                    dev[:, :, cols],
+                    h[b][:].rearrange("p (c d) -> p d c", d=D),
+                    float(D),
+                    hsum[half][:, cols].rearrange("p (o c) -> p o c", o=1).to_broadcast([P, D, 64]),
+                    ALU.mult,
+                    ALU.subtract,
+                )
+                nc.scalar.activation(sq[half][:, :, cols], dev[:, :, cols], ACT.Square, scale=C1)
+
+        def turn_back(qt, half, k):
+            held_qt = sb("qt%d" % half, [P, 128], F32)
+            nc.scalar.copy(held_qt[:], qt[:, 0:128])
+            qb = bank(k, "qn%d" % half)
+            nc.tensor.transpose(qb[:, 0:128], held_qt[:], ident[:])
+            return qb
+
         def spread(half, k):
             qb = bank(k, "q%d" % half)
             for d in range(D):
-                nc.tensor.matmul(qb[:, 0:128], sq[half][:, d, :], ident[:], start=(d == 0), stop=(d == D - 1), is_transpose=True)
+                nc.tensor.matmul(qb[:, 0:128], sq[half][:, D - 1 - d, :], ident[:], start=(d == 0), stop=(d == D - 1), is_transpose=True)
             return qb
 
         def y_sums(y, half):
@@ -190,8 +215,6 @@ def tile_picked_ywien_wien_po_kernel(
             nc.scalar.activation(x0[:], hsum_all[:], ACT.Square, scale=C0)
             return shrink("g0", x0[:], 4, nc.gpsimd)
 
-        gain8 = sb("gain8", [P, PACK], F32)
-        nc.gpsimd.tensor_scalar(gain8[:], gain[:], 1.0 / D, 0.0, ALU.mult, ALU.add)
 
         def along_groups(ap):
             return ap.rearrange("p (o t) -> p o t", o=1).to_broadcast([P, 32, PACK])
@@ -199,17 +222,32 @@ def tile_picked_ywien_wien_po_kernel(
         def by_t(ap):
             return ap.rearrange("p (c t) -> p c t", t=PACK)
 
-        def factors(half, g0, qb):
-            ym = sb("ym%d" % half, [P, 128], F32)
-            nc.gpsimd.tensor_tensor(by_t(ym[:]), by_t(ysum[half][:]), along_groups(gain8[:]), ALU.mult)
-            g1 = shrink("g1_%d" % half, qb[:, 0:128], 2, nc.vector)
+        def slopes(half, qb):
+            q = sb("g1_q%d" % half, [P, 128], F32)
+            r = sb("g1_r%d" % half, [P, 128], F32)
+            nc.scalar.activation(q[:], qb[:, 0:128], ACT.Abs_reciprocal_sqrt, bias=1.0)
+            nc.scalar.activation(r[:], q[:], ACT.Square)
+            g1 = sb("g1_%d" % half, [P, 128], F32)
+            nc.vector.tensor_tensor(
+                g1[:].rearrange("p (b v t) -> p b v t", b=2, t=PACK),
+                qb[:, 0:128].rearrange("p (b t v) -> p b v t", b=2, t=PACK),
+                r[:].rearrange("p (b t v) -> p b v t", b=2, t=PACK),
+                ALU.mult,
+            )
             slope = sb("slope%d" % half, [P, 128], F32)
             nc.vector.tensor_tensor(by_t(slope[:]), by_t(g1[:]), along_groups(gain[:]), ALU.mult)
+            return slope
+
+        def shifts(half, g0, slope):
+            mean = sb("mean%d" % half, [P, 128], F32)
+            nc.gpsimd.tensor_scalar(mean[:], ysum[half][:], 1.0 / D, 0.0, ALU.mult, ALU.add)
+            g0u = sb("g0u%d" % half, [P, 128], F32)
+            nc.gpsimd.tensor_tensor(by_t(g0u[:]), by_t(g0[:, 128 * half : 128 * (half + 1)]), along_groups(gain[:]), ALU.mult)
             diff = sb("diff%d" % half, [P, 128], F32)
-            nc.gpsimd.tensor_tensor(diff[:], g0[:, 128 * half : 128 * (half + 1)], g1[:], ALU.subtract)
+            nc.gpsimd.tensor_tensor(diff[:], g0u[:], slope[:], ALU.subtract)
             shift = sb("shift%d" % half, [P, 128], F32)
-            nc.gpsimd.tensor_tensor(shift[:], diff[:], ym[:], ALU.mult)
-            return slope, shift
+            nc.gpsimd.tensor_tensor(shift[:], diff[:], mean[:], ALU.mult)
+            return shift
 
         def over_group(ap, b):
             return ap[:, 64 * b : 64 * (b + 1)].rearrange("p (v o t) -> p v o t", o=1, t=PACK).to_broadcast([P, GV, D, PACK])
@@ -267,19 +305,20 @@ def tile_picked_ywien_wien_po_kernel(
         h1 = first_product("h", (2, 3), e_g[1], e_gs, 1)
         h_sums(h0, 0)
         deviations(0, (4, 5))
-        h_sums(h1, 1)
+        h_sums_direct(h1, 1)
+        g0 = mean_gain()
         q0 = spread(0, 4)
         gather_scales(0)
         x_g0 = gather_words("x_g0", x_w, 0)
         y0 = first_product("y", (6, 7), x_g0, x_gs, 0)
-        deviations(1, (0, 1))
         gather_scales(1)
         x_g1 = gather_words("x_g1", x_w, 1)
-        q1 = spread(1, 5)
         y1 = first_product("y", (2, 3), x_g1, x_gs, 1)
+        q1 = turn_back(spread(1, 0), 1, 1)
         y_sums(y0, 0)
-        g0 = mean_gain()
-        slope0, shift0 = factors(0, g0, q0)
+        slope0 = slopes(0, q0)
+        shift0 = shifts(0, g0, slope0)
+        slope1 = slopes(1, q1)
         w2_bf = sb("w2_bf", [P, PACK, P, PACK], BF16)
         for a in range(2):
             round_weight(w2_bf, w2_raw[a], a, 0, 32)
@@ -291,7 +330,7 @@ def tile_picked_ywien_wien_po_kernel(
         for c in range(2):
             o.append(second_product(c, shifted(c, scaled(c, y0[c], slope0), shift0), c))
         y_sums(y1, 1)
-        slope1, shift1 = factors(1, g0, q1)
+        shift1 = shifts(1, g0, slope1)
         for c in range(2, 4):
             o.append(second_product(c, shifted(c, scaled(c, y1[c - 2], slope1), shift1), 4 + c))
         for c in range(4):

@@ -129,6 +129,24 @@ def tile_picked_ywien_wien_po_kernel(
                 res.append(dst)
             return res
 
+        def estimate_product(banks, half):
+            res = []
+            for b in range(2):
+                dst = bank(banks[b], "h%d%d" % (half, b))
+                for k in range(2):
+                    cols = slice(P * (2 * b + k), P * (2 * b + k + 1))
+                    nc.tensor.matmul_mx(
+                        out=dst[:, HALF * k : HALF * (k + 1)],
+                        lhsT=w1_c[:, cols].bitcast(FP8X4),
+                        lhsT_scale=w1_s[:, cols],
+                        rhs=e_g[half][:].bitcast(FP8X4),
+                        rhs_scale=e_gs[:, HALF * half : HALF * (half + 1)],
+                        start=True,
+                        stop=True,
+                    )
+                res.append(dst)
+            return res
+
         hsum_all = sb("hsum", [P, 256], F32)
         hsum = [hsum_all[:, 128 * k : 128 * (k + 1)] for k in range(2)]
         hneg = [sb("hneg%d" % k, [P, D, 128], F32) for k in range(2)]
@@ -196,28 +214,27 @@ def tile_picked_ywien_wien_po_kernel(
                     ALU.add,
                 )
 
-        def shrink(name, x, nb, eng):
-            q = sb(name + "_q", [P, 64 * nb], F32)
-            r = sb(name + "_r", [P, 64 * nb], F32)
-            g = sb(name + "_g", [P, 64 * nb], F32)
-            nc.scalar.activation(q[:], x, ACT.Abs_reciprocal_sqrt, bias=1.0)
+        def mean_gain():
+            x0 = sb("x0", [P, 256], F32)
+            q = sb("g0_q", [P, 256], F32)
+            r = sb("g0_r", [P, 256], F32)
+            g = sb("g0_g", [P, 256], F32)
+            nc.scalar.activation(x0[:], hsum_all[:], ACT.Square, scale=C0)
+            nc.scalar.activation(q[:], x0[:], ACT.Abs_reciprocal_sqrt, bias=1.0)
             nc.scalar.activation(r[:], q[:], ACT.Square)
-            eng.tensor_tensor(
-                g[:].rearrange("p (b v t) -> p b v t", b=nb, t=PACK),
-                x.rearrange("p (b t v) -> p b v t", b=nb, t=PACK),
-                r[:].rearrange("p (b t v) -> p b v t", b=nb, t=PACK),
+            nc.gpsimd.tensor_tensor(
+                g[:].rearrange("p (h c t) -> p h c t", h=2, t=PACK),
+                x0[:].rearrange("p (h t c) -> p h c t", h=2, t=PACK),
+                r[:].rearrange("p (h t c) -> p h c t", h=2, t=PACK),
                 ALU.mult,
             )
             return g
 
-        def mean_gain():
-            x0 = sb("x0", [P, 256], F32)
-            nc.scalar.activation(x0[:], hsum_all[:], ACT.Square, scale=C0)
-            return shrink("g0", x0[:], 4, nc.gpsimd)
+        gain8 = sb("gain8", [P, PACK], F32)
+        nc.gpsimd.tensor_scalar(gain8[:], gain[:], 1.0 / D, 0.0, ALU.mult, ALU.add)
 
-
-        def along_groups(ap):
-            return ap.rearrange("p (o t) -> p o t", o=1).to_broadcast([P, 32, PACK])
+        def along_groups(ap, n=32):
+            return ap.rearrange("p (o t) -> p o t", o=1).to_broadcast([P, n, PACK])
 
         def by_t(ap):
             return ap.rearrange("p (c t) -> p c t", t=PACK)
@@ -229,22 +246,20 @@ def tile_picked_ywien_wien_po_kernel(
             nc.scalar.activation(r[:], q[:], ACT.Square)
             g1 = sb("g1_%d" % half, [P, 128], F32)
             nc.vector.tensor_tensor(
-                g1[:].rearrange("p (b v t) -> p b v t", b=2, t=PACK),
-                qb[:, 0:128].rearrange("p (b t v) -> p b v t", b=2, t=PACK),
-                r[:].rearrange("p (b t v) -> p b v t", b=2, t=PACK),
+                by_t(g1[:]),
+                qb[:, 0:128].rearrange("p (t c) -> p c t", t=PACK),
+                r[:].rearrange("p (t c) -> p c t", t=PACK),
                 ALU.mult,
             )
             slope = sb("slope%d" % half, [P, 128], F32)
             nc.vector.tensor_tensor(by_t(slope[:]), by_t(g1[:]), along_groups(gain[:]), ALU.mult)
-            return slope
+            return g1, slope
 
         def shifts(half, g0, slope):
             mean = sb("mean%d" % half, [P, 128], F32)
-            nc.gpsimd.tensor_scalar(mean[:], ysum[half][:], 1.0 / D, 0.0, ALU.mult, ALU.add)
-            g0u = sb("g0u%d" % half, [P, 128], F32)
-            nc.gpsimd.tensor_tensor(by_t(g0u[:]), by_t(g0[:, 128 * half : 128 * (half + 1)]), along_groups(gain[:]), ALU.mult)
+            nc.gpsimd.tensor_tensor(by_t(mean[:]), by_t(ysum[half][:]), along_groups(gain8[:]), ALU.mult)
             diff = sb("diff%d" % half, [P, 128], F32)
-            nc.gpsimd.tensor_tensor(diff[:], g0u[:], slope[:], ALU.subtract)
+            nc.gpsimd.tensor_tensor(diff[:], g0[:, 128 * half : 128 * (half + 1)], slope[:], ALU.subtract)
             shift = sb("shift%d" % half, [P, 128], F32)
             nc.gpsimd.tensor_tensor(shift[:], diff[:], mean[:], ALU.mult)
             return shift
@@ -301,24 +316,25 @@ def tile_picked_ywien_wien_po_kernel(
         def gather_scales(half):
             nc.vector.tensor_copy(x_gs[:, HALF * half : HALF * (half + 1)], x_sc[:].indirect(offsets[:, 16 * half : 16 * (half + 1)]))
 
-        h0 = first_product("h", (0, 1), e_g[0], e_gs, 0)
-        h1 = first_product("h", (2, 3), e_g[1], e_gs, 1)
-        h_sums(h0, 0)
-        deviations(0, (4, 5))
-        h_sums_direct(h1, 1)
-        g0 = mean_gain()
-        q0 = spread(0, 4)
+        h0 = estimate_product((0, 1), 0)
+        h1 = estimate_product((2, 3), 1)
         gather_scales(0)
         x_g0 = gather_words("x_g0", x_w, 0)
-        y0 = first_product("y", (6, 7), x_g0, x_gs, 0)
+        y0 = first_product("y", (4, 5), x_g0, x_gs, 0)
+        h_sums(h0, 0)
+        deviations(0, (0, 1))
         gather_scales(1)
         x_g1 = gather_words("x_g1", x_w, 1)
-        y1 = first_product("y", (2, 3), x_g1, x_gs, 1)
-        q1 = turn_back(spread(1, 0), 1, 1)
+        y1 = first_product("y", (6, 7), x_g1, x_gs, 1)
+        h_sums(h1, 1)
+        q0 = spread(0, 0)
+        g10, slope0 = slopes(0, q0)
+        deviations(1, (2, 3))
+        q1 = spread(1, 2)
+        g0 = mean_gain()
         y_sums(y0, 0)
-        slope0 = slopes(0, q0)
-        shift0 = shifts(0, g0, slope0)
-        slope1 = slopes(1, q1)
+        shift0 = shifts(0, g0, g10)
+        y_sums(y1, 1)
         w2_bf = sb("w2_bf", [P, PACK, P, PACK], BF16)
         for a in range(2):
             round_weight(w2_bf, w2_raw[a], a, 0, 32)
@@ -326,13 +342,13 @@ def tile_picked_ywien_wien_po_kernel(
         w2_c = sb("w2_c", [P, N], U32)
         w2_s = sb("w2_s", [P, N], U8)
         quantize(w2_c[:], w2_s[:], w2_bf[:].rearrange("p t m j -> p (t m j)"))
+        g11, slope1 = slopes(1, q1)
         o = []
         for c in range(2):
-            o.append(second_product(c, shifted(c, scaled(c, y0[c], slope0), shift0), c))
-        y_sums(y1, 1)
-        shift1 = shifts(1, g0, slope1)
+            o.append(second_product(c, shifted(c, scaled(c, y0[c], slope0), shift0), 1 + 2 * c))
+        shift1 = shifts(1, g0, g11)
         for c in range(2, 4):
-            o.append(second_product(c, shifted(c, scaled(c, y1[c - 2], slope1), shift1), 4 + c))
+            o.append(second_product(c, shifted(c, scaled(c, y1[c - 2], slope1), shift1), 2 + c))
         for c in range(4):
             planes(c, o[c])
         for q in range(4):

import math
from contextlib import ExitStack

import concourse.mybir as mybir
from concourse.masks import make_identity

K, T, S, D, H, N = 512, 1024, 512, 8, 512, 512
FLOPS = 3 * 2 * 512 * 512 * 512

F32 = mybir.dt.float32
BF16 = mybir.dt.bfloat16
I32 = mybir.dt.int32
U32 = mybir.dt.uint32
U16 = mybir.dt.uint16
U8 = mybir.dt.uint8
FP8X4 = mybir.dt.float8_e4m3fn_x4
ALU = mybir.AluOpType
ACT = mybir.ActivationFunctionType
AX = mybir.AxisListType

P = 128
PACK = 4
HALF = 256
CH = 128
GV = CH // D
C0 = 1.0 / (D * math.sqrt(0.2))
C1 = 1.0 / (D * math.sqrt(D * 0.3))


def tile_picked_ywien_wien_po_kernel(
    tc, x_words, x_scales, e_words, e_scales, w1, unit, w2, offs, out_0, out_1, out_2
):
    nc = tc.nc
    with ExitStack() as ctx:
        held = ctx.enter_context(tc.tile_pool(name="held", bufs=1))
        psum = ctx.enter_context(tc.psum_pool(name="psum", bufs=1))

        def sb(name, shape, dtype):
            return held.tile(shape, dtype, name=name, align_bytes=64)

        def bank(k, name):
            return psum.tile([P, 512], F32, name=name, tag="bank%d" % k)

        offsets = held.tile([P, S // 16], U16, name="offsets")
        nc.sync.dma_start(offsets[:], offs)

        e_sc = sb("e_sc", [P, T], U8)
        x_sc = sb("x_sc", [P, T], U8)
        nc.vector.memset(e_sc[:].bitcast(I32), 0)
        nc.vector.memset(x_sc[:].bitcast(I32), 0)
        warm_in = sb("warm_in", [P, 1], F32)
        warm_out = sb("warm_out", [P, 1], F32)
        nc.vector.memset(warm_in[:], 1.0)
        nc.scalar.activation(warm_out[:], warm_in[:], ACT.Abs_reciprocal_sqrt)

        def load_weight(name, w, a):
            raw = held.tile([P, PACK, 256], F32, name="%s_raw%d" % (name, a), align_bytes=64)
            nc.sync.dma_start(raw[:], w.rearrange("(p j) c -> p j c", j=PACK)[:, :, 256 * a : 256 * (a + 1)])
            return raw

        def round_weight(dst, raw, a, lo, hi, copy=nc.scalar.copy):
            copy(
                dst[:, :, 64 * a + lo : 64 * a + hi, :].rearrange("p t m j -> p m j t"),
                raw[:, :, PACK * lo : PACK * hi].rearrange("p j (m t) -> p m j t", t=PACK),
            )

        def load_scales(dst, src):
            for q in range(4):
                nc.sync.dma_start(dst[32 * q : 32 * q + 4, :].bitcast(I32), src[0, 4 * q : 4 * q + 4, :].bitcast(I32))

        def load_words(name, src):
            dst = sb(name, [P, T], U32)
            nc.sync.dma_start(dst[:].bitcast(I32), src[0].rearrange("p n t -> p (n t)").bitcast(I32))
            return dst

        w1_raw = [load_weight("w1", w1, 0)]
        load_scales(e_sc, e_scales)
        w1_raw.append(load_weight("w1", w1, 1))
        e_w = load_words("e_w", e_words)
        load_scales(x_sc, x_scales)
        w2_raw = [load_weight("w2", w2, 0)]
        x_w = load_words("x_w", x_words)
        w2_raw.append(load_weight("w2", w2, 1))
        gain = sb("gain", [P, PACK], F32)
        nc.sync.dma_start(gain[:], unit.rearrange("(p t) o -> p (t o)", t=PACK))
        ident = sb("ident", [P, P], F32)
        make_identity(nc, ident[:])

        e_gs = sb("e_gs", [P, S], U8)
        x_gs = sb("x_gs", [P, S], U8)
        nc.vector.tensor_copy(e_gs[:], e_sc[:].indirect(offsets[:]))

        w1_bf = sb("w1_bf", [P, PACK, P, PACK], BF16)
        round_weight(w1_bf, w1_raw[0], 0, 0, 64)
        round_weight(w1_bf, w1_raw[1], 1, 0, 64, nc.vector.tensor_copy)

        def gather_words(name, table, half):
            g = sb(name, [P, HALF], U32)
            nc.vector.tensor_copy(g[:], table[:].indirect(offsets[:, 16 * half : 16 * (half + 1)]))
            return g

        def quantize(codes, scales, values):
            nc.vector.quantize_mx(out=codes.bitcast(FP8X4), scales=scales, in_=values)

        def product(dst, w_codes, w_scales, codes, scales):
            for t in range(PACK):
                cols = slice(P * t, P * (t + 1))
                nc.tensor.matmul_mx(
                    out=dst[:, cols],
                    lhsT=w_codes[:, cols].bitcast(FP8X4),
                    lhsT_scale=w_scales[:, cols],
                    rhs=codes.bitcast(FP8X4),
                    rhs_scale=scales,
                    start=True,
                    stop=True,
                )

        e_g = [gather_words("e_g0", e_w, 0)]
        w1_c = sb("w1_c", [P, N], U32)
        w1_s = sb("w1_s", [P, N], U8)
        quantize(w1_c[:], w1_s[:], w1_bf[:].rearrange("p t m j -> p (t m j)"))
        e_g.append(gather_words("e_g1", e_w, 1))

        def first_product(name, banks, g, gs, half):
            res = []
            for b in range(2):
                dst = bank(banks[b], "%s%d%d" % (name, half, b))
                product(dst, w1_c, w1_s, g[:, CH * b : CH * (b + 1)], gs[:, HALF * half + CH * b : HALF * half + CH * (b + 1)])
                res.append(dst)
            return res

        def estimate_product(banks, half):
            res = []
            for b in range(2):
                dst = bank(banks[b], "h%d%d" % (half, b))
                for k in range(2):
                    cols = slice(P * (2 * b + k), P * (2 * b + k + 1))
                    nc.tensor.matmul_mx(
                        out=dst[:, HALF * k : HALF * (k + 1)],
                        lhsT=w1_c[:, cols].bitcast(FP8X4),
                        lhsT_scale=w1_s[:, cols],
                        rhs=e_g[half][:].bitcast(FP8X4),
                        rhs_scale=e_gs[:, HALF * half : HALF * (half + 1)],
                        start=True,
                        stop=True,
                    )
                res.append(dst)
            return res

        hsum_all = sb("hsum", [P, 256], F32)
        hsum = [hsum_all[:, 128 * k : 128 * (k + 1)] for k in range(2)]
        hneg = [sb("hneg%d" % k, [P, D, 128], F32) for k in range(2)]
        sq = [sb("sq%d" % k, [P, D, 128], F32) for k in range(2)]
        ysum = [sb("ysum%d" % k, [P, 128], F32) for k in range(2)]

        def h_sums(h, half):
            for b in range(2):
                nc.vector.tensor_reduce(
                    hsum[half][:, 64 * b : 64 * (b + 1)], h[b][:].rearrange("p (c d) -> p c d", d=D), AX.X, ALU.add
                )
                o = 1 - b
                nc.scalar.activation(
                    hneg[half][:, :, 64 * o : 64 * (o + 1)], h[o][:].rearrange("p (c d) -> p d c", d=D), ACT.Copy, scale=-8.0
                )

        def deviations(half, banks):
            for u in range(2):
                dh = bank(banks[u], "dh%d%d" % (half, u))
                for d4 in range(4):
                    cols = slice(P * d4, P * (d4 + 1))
                    nc.tensor.matmul(dh[:, cols], hneg[half][:, 4 * u + d4, :], ident[:], start=True, stop=False, is_transpose=True)
                    nc.tensor.matmul(dh[:, cols], hsum[half], ident[:], start=False, stop=True, is_transpose=True)
                nc.scalar.activation(
                    sq[half][:, 4 * u : 4 * (u + 1), :].rearrange("p d c -> p (d c)"), dh[:], ACT.Square, scale=C1
                )

        def h_sums_direct(h, half):
            dev = sb("dev%d" % half, [P, D, 128], F32)
            for b in range(2):
                nc.vector.tensor_reduce(
                    hsum[half][:, 64 * b : 64 * (b + 1)], h[b][:].rearrange("p (c d) -> p c d", d=D), AX.X, ALU.add
                )
            for b in range(2):
                cols = slice(64 * b, 64 * (b + 1))
                nc.vector.scalar_tensor_tensor(
                    dev[:, :, cols],
                    h[b][:].rearrange("p (c d) -> p d c", d=D),
                    float(D),
                    hsum[half][:, cols].rearrange("p (o c) -> p o c", o=1).to_broadcast([P, D, 64]),
                    ALU.mult,
                    ALU.subtract,
                )
                nc.scalar.activation(sq[half][:, :, cols], dev[:, :, cols], ACT.Square, scale=C1)

        def turn_back(qt, half, k):
            held_qt = sb("qt%d" % half, [P, 128], F32)
            nc.scalar.copy(held_qt[:], qt[:, 0:128])
            qb = bank(k, "qn%d" % half)
            nc.tensor.transpose(qb[:, 0:128], held_qt[:], ident[:])
            return qb

        def spread(half, k):
            qb = bank(k, "q%d" % half)
            for d in range(D):
                nc.tensor.matmul(qb[:, 0:128], sq[half][:, D - 1 - d, :], ident[:], start=(d == 0), stop=(d == D - 1), is_transpose=True)
            return qb

        def y_sums(y, half):
            for b in range(2):
                nc.vector.tensor_reduce(
                    ysum[half][:, 64 * b : 64 * (b + 1)].rearrange("p (v t) -> p t v", t=PACK),
                    y[b][:].rearrange("p (t v d) -> p t v d", t=PACK, d=D),
                    AX.X,
                    ALU.add,
                )

        def mean_gain():
            x0 = sb("x0", [P, 256], F32)
            q = sb("g0_q", [P, 256], F32)
            r = sb("g0_r", [P, 256], F32)
            g = sb("g0_g", [P, 256], F32)
            nc.scalar.activation(x0[:], hsum_all[:], ACT.Square, scale=C0)
            nc.scalar.activation(q[:], x0[:], ACT.Abs_reciprocal_sqrt, bias=1.0)
            nc.scalar.activation(r[:], q[:], ACT.Square)
            nc.gpsimd.tensor_tensor(
                g[:].rearrange("p (h c t) -> p h c t", h=2, t=PACK),
                x0[:].rearrange("p (h t c) -> p h c t", h=2, t=PACK),
                r[:].rearrange("p (h t c) -> p h c t", h=2, t=PACK),
                ALU.mult,
            )
            return g

        gain8 = sb("gain8", [P, PACK], F32)
        nc.gpsimd.tensor_scalar(gain8[:], gain[:], 1.0 / D, 0.0, ALU.mult, ALU.add)

        def along_groups(ap, n=32):
            return ap.rearrange("p (o t) -> p o t", o=1).to_broadcast([P, n, PACK])

        def by_t(ap):
            return ap.rearrange("p (c t) -> p c t", t=PACK)

        def slopes(half, qb):
            q = sb("g1_q%d" % half, [P, 128], F32)
            r = sb("g1_r%d" % half, [P, 128], F32)
            nc.scalar.activation(q[:], qb[:, 0:128], ACT.Abs_reciprocal_sqrt, bias=1.0)
            nc.scalar.activation(r[:], q[:], ACT.Square)
            g1 = sb("g1_%d" % half, [P, 128], F32)
            nc.vector.tensor_tensor(
                by_t(g1[:]),
                qb[:, 0:128].rearrange("p (t c) -> p c t", t=PACK),
                r[:].rearrange("p (t c) -> p c t", t=PACK),
                ALU.mult,
            )
            slope = sb("slope%d" % half, [P, 128], F32)
            nc.vector.tensor_tensor(by_t(slope[:]), by_t(g1[:]), along_groups(gain[:]), ALU.mult)
            return g1, slope

        def shifts(half, g0, slope):
            mean = sb("mean%d" % half, [P, 128], F32)
            nc.gpsimd.tensor_tensor(by_t(mean[:]), by_t(ysum[half][:]), along_groups(gain8[:]), ALU.mult)
            diff = sb("diff%d" % half, [P, 128], F32)
            nc.gpsimd.tensor_tensor(diff[:], g0[:, 128 * half : 128 * (half + 1)], slope[:], ALU.subtract)
            shift = sb("shift%d" % half, [P, 128], F32)
            nc.gpsimd.tensor_tensor(shift[:], diff[:], mean[:], ALU.mult)
            return shift

        def over_group(ap, b):
            return ap[:, 64 * b : 64 * (b + 1)].rearrange("p (v o t) -> p v o t", o=1, t=PACK).to_broadcast([P, GV, D, PACK])

        def vdt(ap):
            return ap.rearrange("p (v d t) -> p v d t", d=D, t=PACK)

        def scaled(c, yb, slope):
            u = sb("u%d" % c, [P, 512], F32)
            nc.vector.tensor_tensor(
                vdt(u[:]), yb[:].rearrange("p (t v d) -> p v d t", t=PACK, d=D), over_group(slope, c % 2), ALU.mult
            )
            return u

        def shifted(c, u, shift):
            z = sb("z%d" % c, [P, 512], BF16)
            eng = nc.gpsimd if c in () else nc.vector
            eng.tensor_tensor(vdt(z[:]), vdt(u[:]), over_group(shift, c % 2), ALU.add)
            return z

        out_rows = out_0.rearrange("(p t) j -> p t j", t=PACK)
        o_c = sb("o_c", [P, S], U32)
        o_s = sb("o_s", [P, S], U8)
        out_words = out_1[0].rearrange("p n t -> p (n t)").bitcast(I32)

        def second_product(c, z, k):
            z_c = sb("z_c%d" % c, [P, CH], U32)
            z_s = sb("z_s%d" % c, [P, CH], U8)
            quantize(z_c[:], z_s[:], z[:])
            dst = bank(k, "o%d" % c)
            product(dst, w2_c, w2_s, z_c[:], z_s[:])
            o16 = sb("o16_%d" % c, [P, CH, PACK], BF16)
            o32 = sb("o32_%d" % c, [P, PACK, CH], F32)
            nc.scalar.copy(o32[:].rearrange("p t j -> p (t j)"), dst[:])
            nc.sync.dma_start(out_rows[:, :, CH * c : CH * (c + 1)], o32[:])
            if c in (2,3):
                nc.vector.tensor_copy(
                    o16[:].rearrange("p (c i) t -> p c t i", i=4), o32[:].rearrange("p t (c i) -> p c t i", i=4)
                )
            else:
                nc.scalar.copy(o16[:], dst[:].rearrange("p (t j) -> p j t", t=PACK))
            return o16

        def planes(c, o16):
            cols = slice(CH * c, CH * (c + 1))
            quantize(o_c[:, cols], o_s[:, cols], o16[:].rearrange("p j t -> p (j t)"))
            if c >= 2:
                cols = slice(0, 3 * CH) if c == 2 else cols
                nc.sync.dma_start(out_words[:, cols], o_c[:, cols].bitcast(I32))

        def gather_scales(half):
            nc.vector.tensor_copy(x_gs[:, HALF * half : HALF * (half + 1)], x_sc[:].indirect(offsets[:, 16 * half : 16 * (half + 1)]))

        h0 = estimate_product((0, 1), 0)
        h1 = estimate_product((2, 3), 1)
        gather_scales(0)
        x_g0 = gather_words("x_g0", x_w, 0)
        y0 = first_product("y", (4, 5), x_g0, x_gs, 0)
        h_sums(h0, 0)
        deviations(0, (0, 1))
        gather_scales(1)
        x_g1 = gather_words("x_g1", x_w, 1)
        y1 = first_product("y", (6, 7), x_g1, x_gs, 1)
        h_sums(h1, 1)
        q0 = spread(0, 0)
        g10, slope0 = slopes(0, q0)
        deviations(1, (2, 3))
        q1 = spread(1, 2)
        g0 = mean_gain()
        y_sums(y0, 0)
        shift0 = shifts(0, g0, g10)
        y_sums(y1, 1)
        w2_bf = sb("w2_bf", [P, PACK, P, PACK], BF16)
        for a in range(2):
            round_weight(w2_bf, w2_raw[a], a, 0, 32)
            round_weight(w2_bf, w2_raw[a], a, 32, 64)
        w2_c = sb("w2_c", [P, N], U32)
        w2_s = sb("w2_s", [P, N], U8)
        quantize(w2_c[:], w2_s[:], w2_bf[:].rearrange("p t m j -> p (t m j)"))
        g11, slope1 = slopes(1, q1)
        o = []
        for c in range(2):
            o.append(second_product(c, shifted(c, scaled(c, y0[c], slope0), shift0), 1 + 2 * c))
        shift1 = shifts(1, g0, g11)
        for c in range(2, 4):
            o.append(second_product(c, shifted(c, scaled(c, y1[c - 2], slope1), shift1), 2 + c))
        for c in range(4):
            planes(c, o[c])
        for q in range(4):
            eng = nc.sync if q % 2 == 0 else nc.scalar
            eng.dma_start(out_2[0, 4 * q : 4 * q + 4, :].bitcast(I32), o_s[32 * q : 32 * q + 4, :].bitcast(I32))
